import numpy as np
import ml_dtypes


def mxq(x, axis, fmt="e4m3"):
    dtype, down = {"e4m3": (ml_dtypes.float8_e4m3fn, 7), "e5m2": (ml_dtypes.float8_e5m2, 14)}[fmt]
    v = np.moveaxis(np.asarray(x, np.float32).astype(ml_dtypes.bfloat16).astype(np.float64), axis, -1)
    blocks = v.reshape(v.shape[:-1] + (-1, 32))
    amax = np.abs(blocks).max(-1, keepdims=True)
    byte = np.maximum(np.where(amax > 0, np.frexp(amax)[1] - 1 + 127, 0) - down, 1)
    scale = np.exp2(byte - 127.0)
    codes = (blocks / scale).astype(np.float32).astype(dtype).astype(np.float64)
    return np.moveaxis((codes * scale).reshape(v.shape), -1, axis)


WIDE = False


def mx_kscale(k):
    if not WIDE:
        return np.ones(k)
    levels = np.array([10, -10, 5, -5, 0])
    if k % 512:
        return np.exp2(np.random.permutation(np.resize(levels, k // 32))).repeat(32)
    a = np.empty((k // 512, 16))
    for p in range(k // 512):
        a[p, :8] = np.random.permutation(np.resize(levels, 8))
        for g in range(8):
            far = levels[np.abs(levels - a[p, g]) >= 10]
            a[p, g + 8] = far[np.random.randint(len(far))]
    return np.exp2(a.ravel()).repeat(32)


def f64(x):
    return np.asarray(x).astype(np.float64)


def striped(idx):
    return np.tile(idx.reshape(-1, 16).T, (8, 1)).astype(np.uint16)


def unstriped(offs):
    return offs[:16].T.reshape(-1).astype(np.int64)


def striped8(idx):
    return np.concatenate([v.reshape(-1, 16).T for v in idx]).astype(np.uint16)


def unstriped8(offs):
    return np.stack([offs[16 * g:16 * g + 16].T.reshape(-1) for g in range(8)]).astype(np.int64)


E2M1 = np.array([0.0, 0.5, 1.0, 1.5, 2.0, 3.0, 4.0, 6.0, -0.0, -0.5, -1.0, -1.5, -2.0, -3.0, -4.0, -6.0])


def pack_weight(w, fmt):
    k, n = w.shape
    w = f64(np.asarray(w, np.float32).astype(ml_dtypes.bfloat16)).reshape(k // 32, 32, n)
    amax = np.abs(w).max(1)
    if fmt == "e4m3":
        byte = np.frexp(amax)[1] - 1 + 127 - 7
    else:
        mant, ex = np.frexp(amax / 6.0)
        byte = np.where(mant > 0.5, ex, ex - 1) + 127
    byte = np.clip(np.where(amax > 0, byte, 1), 1, 254)
    scaled = (w * np.exp2(127.0 - byte)[:, None, :]).reshape(k, n).astype(np.float32)
    by_word = np.ascontiguousarray(scaled.reshape(k // 512, 128, 4, n).transpose(0, 1, 3, 2))
    if fmt == "e4m3":
        words = by_word.astype(ml_dtypes.float8_e4m3fn).view(np.uint8)
    else:
        c = by_word.astype(ml_dtypes.float4_e2m1fn).view(np.uint8) & 0xF
        words = (c[..., 0::2] | (c[..., 1::2] << 4)).reshape(k // 512, 128, 2 * n)
    return np.ascontiguousarray(words), np.ascontiguousarray(byte.astype(np.uint8).reshape(k // 512, 16, n))


def unpack_weight(words, scales, fmt):
    g, _, n = scales.shape
    words = np.ascontiguousarray(words).reshape(g, 128, n, -1)
    if fmt == "e4m3":
        vals = words.view(ml_dtypes.float8_e4m3fn).astype(np.float64)
    else:
        nib = np.empty((g, 128, n, 4), np.uint8)
        nib[..., 0::2] = words & 0xF
        nib[..., 1::2] = words >> 4
        vals = E2M1[nib]
    vals = vals * np.repeat(np.exp2(scales.astype(np.float64) - 127.0), 8, axis=1)[..., None]
    return vals.transpose(0, 1, 3, 2).reshape(g * 512, n)


def pack_table(v):
    words, scales = pack_weight(v, "e4m3")
    return np.concatenate([words.reshape(words.shape[0], -1), scales.reshape(scales.shape[0], -1)], axis=1)


def unpack_table(tab):
    g, t = tab.shape[0], tab.shape[1] // 528
    return unpack_weight(tab[:, :512 * t].reshape(g, 128, t, 4), tab[:, 512 * t:].reshape(g, 16, t), "e4m3")


def gelu(v):
    return 0.5 * v * (1.0 + np.tanh(np.sqrt(2.0 / np.pi) * (v + 0.044715 * v**3)))


K, L, M, T, S = 1024, 1024, 512, 1024, 512


def setup_inputs():
    n = np.random.standard_normal
    s1 = mx_kscale(K)[:, None]
    s2 = mx_kscale(L)[:, None]
    p_w4 = pack_weight(n((K, M)) / np.sqrt(K) / s1, "e2m1")
    return {
        "xT": (n((K, T)) * s1).astype(np.float32),
        "w4_words": p_w4[0],
        "w4_scales": p_w4[1],
        "tab": pack_table(n((L, T)) * s2),
        "u": (n((L, M)) / np.sqrt(L) / s2).astype(np.float32),
        "wgt": np.repeat(np.random.uniform(0.5, 2.0, (8, S)), 16, axis=0).astype(np.float32),
        "b": (0.3 * n(512)).astype(np.float32),
        "offs": striped(np.random.permutation(T)[:S]),
        "offs2": striped8(np.stack([np.random.permutation(T)[:S] for _ in range(8)])),
    }


def reference(xT, w4_words, w4_scales, tab, u, wgt, b, offs, offs2):
    idx2 = unstriped8(offs2)
    group = np.arange(K) % 512 // 64
    xg = f64(wgt)[np.arange(K) // 4 % 128] * f64(xT)[np.arange(K)[:, None], idx2[group]]
    xT_ = mxq(xg, 0, "e4m3")
    w4_ = unpack_weight(w4_words, w4_scales, "e2m1")
    tab_ = unpack_table(tab)[:, unstriped(offs)]
    u_ = mxq(f64(u), 0, "e4m3")
    y = w4_.T @ xT_ + u_.T @ tab_
    return gelu(y + f64(b)[:, None])

@@ -1,0 +1,205 @@
+from contextlib import ExitStack
+
+import concourse.mybir as mybir
+from concourse.masks import make_identity
+
+K, L, M, T, S = 1024, 1024, 512, 1024, 512
+FLOPS = 2 * (K + L) * M * S
+
+F32 = mybir.dt.float32
+BF16 = mybir.dt.bfloat16
+I32 = mybir.dt.int32
+U32 = mybir.dt.uint32
+U16 = mybir.dt.uint16
+U8 = mybir.dt.uint8
+FP8X4 = mybir.dt.float8_e4m3fn_x4
+FP4X4 = mybir.dt.float4_e2m1fn_x4
+GELU = mybir.ActivationFunctionType.Gelu_apprx_tanh
+MULT = mybir.AluOpType.mult
+
+P = 128
+PACK = 4
+KP = P * PACK
+
+
+def tile_list_htab_gelu_kernel(tc, xT, w4_words, w4_scales, tab, u, wgt, b, offs, offs2, out):
+    nc = tc.nc
+    with ExitStack() as ctx:
+        keep = ctx.enter_context(tc.tile_pool(name="keep", bufs=1))
+        psum = ctx.enter_context(tc.psum_pool(name="psum", bufs=1))
+
+        def sb(name, shape, dtype, tag=None):
+            return keep.tile(shape, dtype, name=name, tag=tag or name, align_bytes=64)
+
+        offs_sb = sb("offs_sb", [P, S // 16], U16)
+        offs2_sb = sb("offs2_sb", [P, S // 16], U16)
+        tab_words = [sb("tab_words%d" % a, [P, T], I32) for a in range(2)]
+        tab_scales = sb("tab_scales", [P, T], U8)
+        w4_sb = sb("w4_sb", [P, 2, 2 * M], U8)
+        w4_sc = sb("w4_sc", [P, 2, M], U8)
+        wgt_sb = sb("wgt_sb", [P, S], F32)
+        x_planes = [sb("x_plane%d" % i, [P, T], F32) for i in range(8)]
+        b_rows = sb("b_rows", [P, P], F32)
+        ident = sb("ident", [P, P], F32)
+        b_cols = sb("b_cols", [P, 4], F32)
+        warm = sb("warm", [P, 1], F32)
+        picked = [sb("picked%d" % a, [P, PACK, S], F32) for a in range(2)]
+        xg_codes = [sb("xg_codes%d" % a, [P, S], U32) for a in range(2)]
+        xg_scales = {}
+        v_codes = [sb("v_codes%d" % a, [P, S], U32) for a in range(2)]
+        v_scales = sb("v_scales", [P, S], U8)
+        acc = [psum.tile([P, S], F32, name="acc%d" % c) for c in range(4)]
+        b_ps = psum.tile([P, P], F32, name="b_ps")
+        u_raw = {}
+        u_codes = {}
+        u_scales = {}
+
+        nc.gpsimd.memset(tab_scales[:].bitcast(I32), 0)
+        nc.vector.memset(w4_sc[:].bitcast(I32), 0)
+        nc.vector.memset(b_rows[:], 0.0)
+
+        def load_small():
+            scale_rows = tab[:, KP * T :].rearrange("a (q t) -> a q t", t=T).bitcast(I32)
+            for q in range(4):
+                nc.scalar.dma_start(out=tab_scales[:].bitcast(I32)[32 * q + 4 : 32 * q + 12, :], in_=scale_rows[:, 4 * q : 4 * q + 4, :])
+            for q in range(4):
+                nc.gpsimd.dma_start(
+                    out=w4_sc[:].bitcast(I32)[32 * q : 32 * q + 4, :, :],
+                    in_=w4_scales[:, 4 * q : 4 * q + 4, :].rearrange("a r n -> r a n").bitcast(I32),
+                )
+            nc.gpsimd.dma_start(out=b_rows[0:4, :], in_=b.rearrange("(c p) -> c p", p=P))
+
+        def load_tab(a):
+            nc.sync.dma_start(out=tab_words[a][:], in_=tab[a, 0 : KP * T].rearrange("(p x) -> p x", p=P).bitcast(I32))
+
+        def load_x(i):
+            a, t = divmod(i, PACK)
+            nc.sync.dma_start(out=x_planes[i][:], in_=xT[KP * a : KP * (a + 1), :].rearrange("(p t) x -> p t x", t=PACK)[:, t, :])
+
+        def load_u(a, n0, n1):
+            u_raw[a, n0] = sb("u_raw%d_%d" % (a, n0), [P, PACK, n1 - n0], F32)
+            nc.sync.dma_start(out=u_raw[a, n0][:], in_=u[KP * a : KP * (a + 1), n0:n1].rearrange("(p t) n -> p t n", t=PACK))
+
+        def load_w4():
+            nc.sync.dma_start(out=w4_sb[:].bitcast(I32), in_=w4_words.rearrange("a p x -> p a x").bitcast(I32))
+
+        def weave(engine, name, src, width):
+            woven = sb(name, [P, width, PACK], BF16)
+            dst = woven[:].rearrange("p (c i) t -> p c t i", i=4)
+            rd = src.rearrange("p t (c i) -> p c t i", i=4)
+            if engine == "S":
+                nc.scalar.copy(dst, rd)
+            else:
+                nc.vector.tensor_copy(dst, rd)
+            return woven
+
+        def gather_x(i, j0, j1):
+            a, t = divmod(i, PACK)
+            nc.vector.tensor_tensor(picked[a][:, t, j0:j1], x_planes[i][:].indirect(offs2_sb[:, j0 // 16 : j1 // 16]), wgt_sb[:, j0:j1], MULT)
+
+        def quant_x(engine, a, j0, j1, tag=None):
+            if a not in xg_scales:
+                xg_scales[a] = sb("xg_scales%d" % a, [P, S], U8, tag)
+            woven = weave(engine, "x_woven%d_%d" % (a, j0), picked[a][:, :, j0:j1], j1 - j0)
+            nc.vector.quantize_mx(out=xg_codes[a][:, j0:j1].bitcast(FP8X4), scales=xg_scales[a][:, j0:j1], in_=woven[:].rearrange("p w t -> p (w t)"))
+
+        def quant_u(engine, a, n0, n1, tag=None):
+            woven = weave(engine, "u_woven%d_%d" % (a, n0), u_raw[a, n0][:], n1 - n0)
+            codes = sb("u_codes%d_%d" % (a, n0), [P, n1 - n0], U32)
+            scales = sb("u_scales%d_%d" % (a, n0), [P, n1 - n0], U8, tag)
+            nc.vector.quantize_mx(out=codes[:].bitcast(FP8X4), scales=scales[:], in_=woven[:].rearrange("p w t -> p (w t)"))
+            for n in range(n0, n1, P):
+                u_codes[a, n // P] = codes[:, n - n0 : n - n0 + P]
+                u_scales[a, n // P] = scales[:, n - n0 : n - n0 + P]
+
+        def gather_tab(a):
+            nc.vector.tensor_copy(v_codes[a][:], tab_words[a][:].bitcast(U32).indirect(offs_sb[:]))
+
+        def gather_scales():
+            nc.vector.tensor_copy(v_scales[:], tab_scales[:].indirect(offs_sb[:]))
+
+        done = [[] for c in range(4)]
+
+        def mm(kind, a, c):
+            first = len(done[c]) == 0
+            done[c].append((kind, a))
+            last = len(done[c]) == 4
+            if kind == "x":
+                nc.tensor.matmul_mx(
+                    out=acc[c][:],
+                    lhsT=w4_sb[:, a, 2 * P * c : 2 * P * (c + 1)].bitcast(FP4X4),
+                    lhsT_scale=w4_sc[:, a, P * c : P * (c + 1)],
+                    rhs=xg_codes[a][:].bitcast(FP8X4),
+                    rhs_scale=xg_scales[a][:],
+                    start=first,
+                    stop=last,
+                )
+            else:
+                nc.tensor.matmul_mx(
+                    out=acc[c][:],
+                    lhsT=u_codes[a, c].bitcast(FP8X4),
+                    lhsT_scale=u_scales[a, c],
+                    rhs=v_codes[a][:].bitcast(FP8X4),
+                    rhs_scale=v_scales[4 + 4 * a : P, :],
+                    start=first,
+                    stop=last,
+                )
+
+        def finish(c, tag=None):
+            y = sb("y%d" % c, [P, S], F32, tag)
+            nc.scalar.activation(y[:], acc[c][:], GELU, bias=b_cols[:, c : c + 1])
+            nc.sync.dma_start(out=out[P * c : P * (c + 1), :], in_=y[:])
+
+        nc.sync.dma_start(offs_sb[:], offs)
+        nc.sync.dma_start(offs2_sb[:], offs2)
+        load_small()
+        make_identity(nc, ident[:])
+        nc.scalar.activation(warm[:], ident[:, 0:1], GELU)
+        nc.tensor.transpose(b_ps[:], b_rows[:], ident[:])
+        nc.scalar.copy(b_cols[:], b_ps[:, 0:4])
+
+        nc.sync.dma_start(out=wgt_sb[:], in_=wgt)
+        for i in range(6):
+            load_x(i)
+        load_u(0, 0, 256)
+        load_x(6)
+        load_w4()
+        load_x(7)
+        load_tab(0)
+        load_u(1, 0, 256)
+        load_tab(1)
+        load_u(0, 256, 512)
+        load_u(1, 256, 384)
+        load_u(1, 384, 512)
+        gather_scales()
+        for i in range(4):
+            gather_x(i, 0, S)
+        quant_x("S", 0, 0, S)
+        quant_u("S", 0, 0, 256)
+        for i in range(4, 7):
+            gather_x(i, 0, S)
+        gather_x(7, 0, 256)
+        gather_x(7, 256, S)
+        gather_tab(0)
+        quant_x("S", 1, 0, 256, "tab_words0")
+        quant_x("S", 1, 256, S)
+        gather_tab(1)
+        quant_u("S", 1, 0, 256, "tab_words1")
+        quant_u("S", 0, 256, 512)
+        quant_u("V", 1, 256, 384)
+        quant_u("V", 1, 384, 512)
+        for c in range(4):
+            mm("x", 0, c)
+        for c in range(2):
+            mm("u", 0, c)
+        for c in range(2):
+            mm("x", 1, c)
+            mm("u", 1, c)
+        for c in range(2, 4):
+            mm("x", 1, c)
+        finish(0, "u_raw0_256")
+        finish(1)
+        for c in range(2, 4):
+            mm("u", 0, c)
+            mm("u", 1, c)
+            finish(c)

@@ -58,16 +58,22 @@ def tile_list_htab_gelu_kernel(tc, xT, w4_words, w4_scales, tab, u, wgt, b, offs
         nc.vector.memset(w4_sc[:].bitcast(I32), 0)
         nc.vector.memset(b_rows[:], 0.0)
 
-        def load_small():
+        def load_tab_scales(q):
             scale_rows = tab[:, KP * T :].rearrange("a (q t) -> a q t", t=T).bitcast(I32)
-            for q in range(4):
-                nc.scalar.dma_start(out=tab_scales[:].bitcast(I32)[32 * q + 4 : 32 * q + 12, :], in_=scale_rows[:, 4 * q : 4 * q + 4, :])
-            for q in range(4):
-                nc.gpsimd.dma_start(
-                    out=w4_sc[:].bitcast(I32)[32 * q : 32 * q + 4, :, :],
-                    in_=w4_scales[:, 4 * q : 4 * q + 4, :].rearrange("a r n -> r a n").bitcast(I32),
-                )
-            nc.gpsimd.dma_start(out=b_rows[0:4, :], in_=b.rearrange("(c p) -> c p", p=P))
+            nc.scalar.dma_start(out=tab_scales[:].bitcast(I32)[32 * q + 4 : 32 * q + 12, :], in_=scale_rows[:, 4 * q : 4 * q + 4, :])
+
+        def load_w4_scales(q):
+            nc.sync.dma_start(
+                out=w4_sc[:].bitcast(I32)[32 * q : 32 * q + 4, :, :],
+                in_=w4_scales[:, 4 * q : 4 * q + 4, :].rearrange("a r n -> r a n").bitcast(I32),
+            )
+
+        def load_b():
+            nc.sync.dma_start(out=b_rows[0:4, :], in_=b.rearrange("(c p) -> c p", p=P))
+
+        def turn_b():
+            nc.tensor.transpose(b_ps[:], b_rows[:], ident[:])
+            nc.scalar.copy(b_cols[:], b_ps[:, 0:4])
 
         def load_tab(a):
             nc.sync.dma_start(out=tab_words[a][:], in_=tab[a, 0 : KP * T].rearrange("(p x) -> p x", p=P).bitcast(I32))
@@ -150,41 +156,47 @@ def tile_list_htab_gelu_kernel(tc, xT, w4_words, w4_scales, tab, u, wgt, b, offs
             nc.scalar.activation(y[:], acc[c][:], GELU, bias=b_cols[:, c : c + 1])
             nc.sync.dma_start(out=out[P * c : P * (c + 1), :], in_=y[:])
 
-        nc.sync.dma_start(offs_sb[:], offs)
-        nc.sync.dma_start(offs2_sb[:], offs2)
-        load_small()
         make_identity(nc, ident[:])
-        nc.scalar.activation(warm[:], ident[:, 0:1], GELU)
-        nc.tensor.transpose(b_ps[:], b_rows[:], ident[:])
-        nc.scalar.copy(b_cols[:], b_ps[:, 0:4])
-
+        nc.sync.dma_start(offs_sb[:], offs)
         nc.sync.dma_start(out=wgt_sb[:], in_=wgt)
-        for i in range(6):
+        nc.sync.dma_start(offs2_sb[:], offs2)
+        for q in range(4):
+            load_tab_scales(q)
+        nc.scalar.activation(warm[:], ident[:, 0:1], GELU)
+        load_x(0)
+        load_x(1)
+        load_b()
+        turn_b()
+        load_x(2)
+        load_w4_scales(0)
+        for i in range(3, 6):
             load_x(i)
-        load_u(0, 0, 256)
+        load_w4_scales(1)
         load_x(6)
-        load_w4()
+        load_w4_scales(2)
+        load_w4_scales(3)
+        load_u(0, 0, 256)
         load_x(7)
         load_tab(0)
-        load_u(1, 0, 256)
+        load_w4()
         load_tab(1)
+        load_u(1, 0, 256)
         load_u(0, 256, 512)
         load_u(1, 256, 384)
         load_u(1, 384, 512)
         gather_scales()
-        for i in range(4):
+        for i in range(6):
             gather_x(i, 0, S)
         quant_x("S", 0, 0, S)
+        gather_x(6, 0, S)
         quant_u("S", 0, 0, 256)
-        for i in range(4, 7):
-            gather_x(i, 0, S)
         gather_x(7, 0, 256)
         gather_x(7, 256, S)
         gather_tab(0)
-        quant_x("S", 1, 0, 256, "tab_words0")
+        quant_x("S", 1, 0, 256)
         quant_x("S", 1, 256, S)
         gather_tab(1)
-        quant_u("S", 1, 0, 256, "tab_words1")
+        quant_u("S", 1, 0, 256)
         quant_u("S", 0, 256, 512)
         quant_u("V", 1, 256, 384)
         quant_u("V", 1, 384, 512)
@@ -192,11 +204,10 @@ def tile_list_htab_gelu_kernel(tc, xT, w4_words, w4_scales, tab, u, wgt, b, offs
             mm("x", 0, c)
         for c in range(2):
             mm("u", 0, c)
+        for c in range(4):
+            mm("x", 1, c)
         for c in range(2):
-            mm("x", 1, c)
             mm("u", 1, c)
-        for c in range(2, 4):
-            mm("x", 1, c)
         finish(0, "u_raw0_256")
         finish(1)
         for c in range(2, 4):

@@ -51,6 +51,7 @@ def tile_list_htab_gelu_kernel(tc, xT, w4_words, w4_scales, tab, u, wgt, b, offs
         acc = [psum.tile([P, S], F32, name="acc%d" % c) for c in range(4)]
         b_ps = psum.tile([P, P], F32, name="b_ps")
         u_raw = {}
+        ys = {}
         u_codes = {}
         u_scales = {}
 
@@ -58,9 +59,9 @@ def tile_list_htab_gelu_kernel(tc, xT, w4_words, w4_scales, tab, u, wgt, b, offs
         nc.vector.memset(w4_sc[:].bitcast(I32), 0)
         nc.vector.memset(b_rows[:], 0.0)
 
-        def load_tab_scales(q):
+        def load_tab_scales(q, queue):
             scale_rows = tab[:, KP * T :].rearrange("a (q t) -> a q t", t=T).bitcast(I32)
-            nc.scalar.dma_start(out=tab_scales[:].bitcast(I32)[32 * q + 4 : 32 * q + 12, :], in_=scale_rows[:, 4 * q : 4 * q + 4, :])
+            queue.dma_start(out=tab_scales[:].bitcast(I32)[32 * q + 4 : 32 * q + 12, :], in_=scale_rows[:, 4 * q : 4 * q + 4, :])
 
         def load_w4_scales(q):
             nc.sync.dma_start(
@@ -151,33 +152,29 @@ def tile_list_htab_gelu_kernel(tc, xT, w4_words, w4_scales, tab, u, wgt, b, offs
                     stop=last,
                 )
 
-        def finish(c, tag=None):
-            y = sb("y%d" % c, [P, S], F32, tag)
-            nc.scalar.activation(y[:], acc[c][:], GELU, bias=b_cols[:, c : c + 1])
-            nc.sync.dma_start(out=out[P * c : P * (c + 1), :], in_=y[:])
+        def finish(c, y):
+            ys[c, 0] = y
+            nc.scalar.activation(y, acc[c][:], GELU, bias=b_cols[:, c : c + 1])
+            nc.sync.dma_start(out=out[P * c : P * (c + 1), :], in_=y)
 
         make_identity(nc, ident[:])
         nc.sync.dma_start(offs_sb[:], offs)
         nc.sync.dma_start(out=wgt_sb[:], in_=wgt)
         nc.sync.dma_start(offs2_sb[:], offs2)
         for q in range(4):
-            load_tab_scales(q)
+            load_tab_scales(q, nc.scalar)
         nc.scalar.activation(warm[:], ident[:, 0:1], GELU)
         load_x(0)
         load_x(1)
         load_b()
         turn_b()
-        load_x(2)
-        load_w4_scales(0)
-        for i in range(3, 6):
+        for i in range(2, 7):
             load_x(i)
-        load_w4_scales(1)
-        load_x(6)
-        load_w4_scales(2)
-        load_w4_scales(3)
         load_u(0, 0, 256)
         load_x(7)
         load_tab(0)
+        for q in range(4):
+            load_w4_scales(q)
         load_w4()
         load_tab(1)
         load_u(1, 0, 256)
@@ -189,9 +186,9 @@ def tile_list_htab_gelu_kernel(tc, xT, w4_words, w4_scales, tab, u, wgt, b, offs
             gather_x(i, 0, S)
         quant_x("S", 0, 0, S)
         gather_x(6, 0, S)
-        quant_u("S", 0, 0, 256)
         gather_x(7, 0, 256)
         gather_x(7, 256, S)
+        quant_u("S", 0, 0, 256)
         gather_tab(0)
         quant_x("S", 1, 0, 256)
         quant_x("S", 1, 256, S)
@@ -208,9 +205,13 @@ def tile_list_htab_gelu_kernel(tc, xT, w4_words, w4_scales, tab, u, wgt, b, offs
             mm("x", 1, c)
         for c in range(2):
             mm("u", 1, c)
-        finish(0, "u_raw0_256")
-        finish(1)
-        for c in range(2, 4):
-            mm("u", 0, c)
-            mm("u", 1, c)
-            finish(c)
+        y_first = sb("y_first", [P, 2 * S], F32, "u_raw0_256")
+        finish(0, y_first[:, 0:S])
+        finish(1, y_first[:, S : 2 * S])
+        mm("u", 1, 2)
+        mm("u", 0, 2)
+        mm("u", 0, 3)
+        mm("u", 1, 3)
+        y_last = sb("y_last", [P, 2 * S], F32)
+        finish(2, y_last[:, 0:S])
+        finish(3, y_last[:, S : 2 * S])

@@ -19,7 +19,17 @@ MULT = mybir.AluOpType.mult
 
 P = 128
 PACK = 4
-KP = P * PACK
+K_PASS = P * PACK
+PASSES = K // K_PASS
+PLANES = PASSES * PACK
+N_TILES = M // P
+QUADRANTS = 4
+QUADRANT = P // QUADRANTS
+SCALE_ROWS = 4
+PER_COLUMN = 16
+LINE = 4
+M_HALF = M // 2
+S_HALF = S // 2
 
 
 def tile_list_htab_gelu_kernel(tc, xT, w4_words, w4_scales, tab, u, wgt, b, offs, offs2, out):
@@ -28,190 +38,176 @@ def tile_list_htab_gelu_kernel(tc, xT, w4_words, w4_scales, tab, u, wgt, b, offs
         keep = ctx.enter_context(tc.tile_pool(name="keep", bufs=1))
         psum = ctx.enter_context(tc.psum_pool(name="psum", bufs=1))
 
-        def sb(name, shape, dtype, tag=None):
+        def sbuf(name, shape, dtype, tag=None):
             return keep.tile(shape, dtype, name=name, tag=tag or name, align_bytes=64)
 
-        offs_sb = sb("offs_sb", [P, S // 16], U16)
-        offs2_sb = sb("offs2_sb", [P, S // 16], U16)
-        tab_words = [sb("tab_words%d" % a, [P, T], I32) for a in range(2)]
-        tab_scales = sb("tab_scales", [P, T], U8)
-        w4_sb = sb("w4_sb", [P, 2, 2 * M], U8)
-        w4_sc = sb("w4_sc", [P, 2, M], U8)
-        wgt_sb = sb("wgt_sb", [P, S], F32)
-        x_planes = [sb("x_plane%d" % i, [P, T], F32) for i in range(8)]
-        b_rows = sb("b_rows", [P, P], F32)
-        ident = sb("ident", [P, P], F32)
-        b_cols = sb("b_cols", [P, 4], F32)
-        warm = sb("warm", [P, 1], F32)
-        picked = [sb("picked%d" % a, [P, PACK, S], F32) for a in range(2)]
-        xg_codes = [sb("xg_codes%d" % a, [P, S], U32) for a in range(2)]
-        xg_scales = {}
-        v_codes = [sb("v_codes%d" % a, [P, S], U32) for a in range(2)]
-        v_scales = sb("v_scales", [P, S], U8)
-        acc = [psum.tile([P, S], F32, name="acc%d" % c) for c in range(4)]
+        offs_sb = sbuf("offs_sb", [P, S // PER_COLUMN], U16)
+        offs2_sb = sbuf("offs2_sb", [P, S // PER_COLUMN], U16)
+        tab_words = [sbuf("tab_words%d" % a, [P, T], I32) for a in range(PASSES)]
+        tab_scales = sbuf("tab_scales", [P, T], U8)
+        w4_sb = sbuf("w4_sb", [P, PASSES, 2 * M], U8)
+        w4_sc = sbuf("w4_sc", [P, PASSES, M], U8)
+        wgt_sb = sbuf("wgt_sb", [P, S], F32)
+        x_planes = [sbuf("x_plane%d" % i, [P, T], F32) for i in range(PLANES)]
+        b_rows = sbuf("b_rows", [P, P], F32)
+        ident = sbuf("ident", [P, P], F32)
+        b_cols = sbuf("b_cols", [P, N_TILES], F32)
+        warm = sbuf("warm", [P, 1], F32)
+        picked = [sbuf("picked%d" % a, [P, PACK, S], F32) for a in range(PASSES)]
+        xg_codes = [sbuf("xg_codes%d" % a, [P, S], U32) for a in range(PASSES)]
+        v_codes = [sbuf("v_codes%d" % a, [P, S], U32) for a in range(PASSES)]
+        v_scales = sbuf("v_scales", [P, S], U8)
+        xg_scales = [sbuf("xg_scales%d" % a, [P, S], U8) for a in range(PASSES)]
+        acc = [psum.tile([P, S], F32, name="acc%d" % c) for c in range(N_TILES)]
         b_ps = psum.tile([P, P], F32, name="b_ps")
         u_raw = {}
-        ys = {}
         u_codes = {}
         u_scales = {}
 
-        nc.gpsimd.memset(tab_scales[:].bitcast(I32), 0)
-        nc.vector.memset(w4_sc[:].bitcast(I32), 0)
-        nc.vector.memset(b_rows[:], 0.0)
-
-        def load_tab_scales(q, queue):
-            scale_rows = tab[:, KP * T :].rearrange("a (q t) -> a q t", t=T).bitcast(I32)
-            queue.dma_start(out=tab_scales[:].bitcast(I32)[32 * q + 4 : 32 * q + 12, :], in_=scale_rows[:, 4 * q : 4 * q + 4, :])
+        def load_tab_scales(q):
+            rows = tab[:, K_PASS * T :].rearrange("a (r t) -> a r t", t=T).bitcast(I32)
+            first = QUADRANT * q + SCALE_ROWS
+            nc.sync.dma_start(
+                out=tab_scales[:].bitcast(I32)[first : first + PASSES * SCALE_ROWS, :],
+                in_=rows[:, SCALE_ROWS * q : SCALE_ROWS * (q + 1), :],
+            )
 
         def load_w4_scales(q):
             nc.sync.dma_start(
-                out=w4_sc[:].bitcast(I32)[32 * q : 32 * q + 4, :, :],
-                in_=w4_scales[:, 4 * q : 4 * q + 4, :].rearrange("a r n -> r a n").bitcast(I32),
+                out=w4_sc[:].bitcast(I32)[QUADRANT * q : QUADRANT * q + SCALE_ROWS, :, :],
+                in_=w4_scales[:, SCALE_ROWS * q : SCALE_ROWS * (q + 1), :].rearrange("a r n -> r a n").bitcast(I32),
             )
 
-        def load_b():
-            nc.sync.dma_start(out=b_rows[0:4, :], in_=b.rearrange("(c p) -> c p", p=P))
+        def load_tab_words(a):
+            nc.sync.dma_start(out=tab_words[a][:], in_=tab[a, 0 : K_PASS * T].rearrange("(p x) -> p x", p=P).bitcast(I32))
 
-        def turn_b():
-            nc.tensor.transpose(b_ps[:], b_rows[:], ident[:])
-            nc.scalar.copy(b_cols[:], b_ps[:, 0:4])
-
-        def load_tab(a):
-            nc.sync.dma_start(out=tab_words[a][:], in_=tab[a, 0 : KP * T].rearrange("(p x) -> p x", p=P).bitcast(I32))
-
-        def load_x(i):
+        def load_plane(i):
             a, t = divmod(i, PACK)
-            nc.sync.dma_start(out=x_planes[i][:], in_=xT[KP * a : KP * (a + 1), :].rearrange("(p t) x -> p t x", t=PACK)[:, t, :])
+            rows = xT[K_PASS * a : K_PASS * (a + 1), :].rearrange("(p t) x -> p t x", t=PACK)
+            nc.sync.dma_start(out=x_planes[i][:], in_=rows[:, t, :])
 
         def load_u(a, n0, n1):
-            u_raw[a, n0] = sb("u_raw%d_%d" % (a, n0), [P, PACK, n1 - n0], F32)
-            nc.sync.dma_start(out=u_raw[a, n0][:], in_=u[KP * a : KP * (a + 1), n0:n1].rearrange("(p t) n -> p t n", t=PACK))
+            u_raw[a, n0] = sbuf("u_raw%d_%d" % (a, n0), [P, PACK, n1 - n0], F32)
+            rows = u[K_PASS * a : K_PASS * (a + 1), n0:n1].rearrange("(p t) n -> p t n", t=PACK)
+            nc.sync.dma_start(out=u_raw[a, n0][:], in_=rows)
 
-        def load_w4():
-            nc.sync.dma_start(out=w4_sb[:].bitcast(I32), in_=w4_words.rearrange("a p x -> p a x").bitcast(I32))
+        def interleave(copy, name, src, width):
+            woven = sbuf(name, [P, width, PACK], BF16)
+            copy(woven[:].rearrange("p (c i) t -> p c t i", i=LINE), src.rearrange("p t (c i) -> p c t i", i=LINE))
+            return woven[:].rearrange("p w t -> p (w t)")
 
-        def weave(engine, name, src, width):
-            woven = sb(name, [P, width, PACK], BF16)
-            dst = woven[:].rearrange("p (c i) t -> p c t i", i=4)
-            rd = src.rearrange("p t (c i) -> p c t i", i=4)
-            if engine == "S":
-                nc.scalar.copy(dst, rd)
-            else:
-                nc.vector.tensor_copy(dst, rd)
-            return woven
-
-        def gather_x(i, j0, j1):
+        def gather_plane(i, j0, j1):
             a, t = divmod(i, PACK)
-            nc.vector.tensor_tensor(picked[a][:, t, j0:j1], x_planes[i][:].indirect(offs2_sb[:, j0 // 16 : j1 // 16]), wgt_sb[:, j0:j1], MULT)
+            window = x_planes[i][:].indirect(offs2_sb[:, j0 // PER_COLUMN : j1 // PER_COLUMN])
+            nc.vector.tensor_tensor(picked[a][:, t, j0:j1], window, wgt_sb[:, j0:j1], MULT)
 
-        def quant_x(engine, a, j0, j1, tag=None):
-            if a not in xg_scales:
-                xg_scales[a] = sb("xg_scales%d" % a, [P, S], U8, tag)
-            woven = weave(engine, "x_woven%d_%d" % (a, j0), picked[a][:, :, j0:j1], j1 - j0)
-            nc.vector.quantize_mx(out=xg_codes[a][:, j0:j1].bitcast(FP8X4), scales=xg_scales[a][:, j0:j1], in_=woven[:].rearrange("p w t -> p (w t)"))
+        def quantise_xg(a, j0, j1):
+            woven = interleave(nc.scalar.copy, "x_woven%d_%d" % (a, j0), picked[a][:, :, j0:j1], j1 - j0)
+            nc.vector.quantize_mx(out=xg_codes[a][:, j0:j1].bitcast(FP8X4), scales=xg_scales[a][:, j0:j1], in_=woven)
 
-        def quant_u(engine, a, n0, n1, tag=None):
-            woven = weave(engine, "u_woven%d_%d" % (a, n0), u_raw[a, n0][:], n1 - n0)
-            codes = sb("u_codes%d_%d" % (a, n0), [P, n1 - n0], U32)
-            scales = sb("u_scales%d_%d" % (a, n0), [P, n1 - n0], U8, tag)
-            nc.vector.quantize_mx(out=codes[:].bitcast(FP8X4), scales=scales[:], in_=woven[:].rearrange("p w t -> p (w t)"))
+        def quantise_u(copy, a, n0, n1):
+            woven = interleave(copy, "u_woven%d_%d" % (a, n0), u_raw[a, n0][:], n1 - n0)
+            codes = sbuf("u_codes%d_%d" % (a, n0), [P, n1 - n0], U32)
+            scales = sbuf("u_scales%d_%d" % (a, n0), [P, n1 - n0], U8)
+            nc.vector.quantize_mx(out=codes[:].bitcast(FP8X4), scales=scales[:], in_=woven)
             for n in range(n0, n1, P):
                 u_codes[a, n // P] = codes[:, n - n0 : n - n0 + P]
                 u_scales[a, n // P] = scales[:, n - n0 : n - n0 + P]
 
-        def gather_tab(a):
+        def gather_tab_words(a):
             nc.vector.tensor_copy(v_codes[a][:], tab_words[a][:].bitcast(U32).indirect(offs_sb[:]))
 
-        def gather_scales():
-            nc.vector.tensor_copy(v_scales[:], tab_scales[:].indirect(offs_sb[:]))
+        def multiply_heads(a, c):
+            nc.tensor.matmul_mx(
+                out=acc[c][:],
+                lhsT=w4_sb[:, a, 2 * P * c : 2 * P * (c + 1)].bitcast(FP4X4),
+                lhsT_scale=w4_sc[:, a, P * c : P * (c + 1)],
+                rhs=xg_codes[a][:].bitcast(FP8X4),
+                rhs_scale=xg_scales[a][:],
+                start=(a == 0),
+                stop=False,
+            )
 
-        done = [[] for c in range(4)]
-
-        def mm(kind, a, c):
-            first = len(done[c]) == 0
-            done[c].append((kind, a))
-            last = len(done[c]) == 4
-            if kind == "x":
-                nc.tensor.matmul_mx(
-                    out=acc[c][:],
-                    lhsT=w4_sb[:, a, 2 * P * c : 2 * P * (c + 1)].bitcast(FP4X4),
-                    lhsT_scale=w4_sc[:, a, P * c : P * (c + 1)],
-                    rhs=xg_codes[a][:].bitcast(FP8X4),
-                    rhs_scale=xg_scales[a][:],
-                    start=first,
-                    stop=last,
-                )
-            else:
-                nc.tensor.matmul_mx(
-                    out=acc[c][:],
-                    lhsT=u_codes[a, c].bitcast(FP8X4),
-                    lhsT_scale=u_scales[a, c],
-                    rhs=v_codes[a][:].bitcast(FP8X4),
-                    rhs_scale=v_scales[4 + 4 * a : P, :],
-                    start=first,
-                    stop=last,
-                )
+        def multiply_table(a, c, closes):
+            nc.tensor.matmul_mx(
+                out=acc[c][:],
+                lhsT=u_codes[a, c].bitcast(FP8X4),
+                lhsT_scale=u_scales[a, c],
+                rhs=v_codes[a][:].bitcast(FP8X4),
+                rhs_scale=v_scales[SCALE_ROWS * (a + 1) : P, :],
+                start=False,
+                stop=closes,
+            )
 
         def finish(c, y):
-            ys[c, 0] = y
             nc.scalar.activation(y, acc[c][:], GELU, bias=b_cols[:, c : c + 1])
             nc.sync.dma_start(out=out[P * c : P * (c + 1), :], in_=y)
 
+        nc.gpsimd.memset(tab_scales[:].bitcast(I32), 0)
+        nc.vector.memset(w4_sc[:].bitcast(I32), 0)
+        nc.vector.memset(b_rows[:], 0.0)
         make_identity(nc, ident[:])
+
         nc.sync.dma_start(offs_sb[:], offs)
         nc.sync.dma_start(out=wgt_sb[:], in_=wgt)
-        nc.sync.dma_start(offs2_sb[:], offs2)
-        for q in range(4):
-            load_tab_scales(q, nc.scalar)
+        for q in range(QUADRANTS):
+            load_tab_scales(q)
         nc.scalar.activation(warm[:], ident[:, 0:1], GELU)
-        load_x(0)
-        load_x(1)
-        load_b()
-        turn_b()
-        for i in range(2, 7):
-            load_x(i)
-        load_u(0, 0, 256)
-        load_x(7)
-        load_tab(0)
-        for q in range(4):
+        load_plane(0)
+        nc.sync.dma_start(offs2_sb[:], offs2)
+        load_plane(1)
+        nc.sync.dma_start(out=b_rows[0:N_TILES, :], in_=b.rearrange("(c p) -> c p", p=P))
+        nc.tensor.transpose(b_ps[:], b_rows[:], ident[:])
+        nc.scalar.copy(b_cols[:], b_ps[:, 0:N_TILES])
+        last_plane = PLANES - 1
+        for i in range(2, last_plane):
+            load_plane(i)
+        load_u(0, 0, M_HALF)
+        load_plane(last_plane)
+        load_tab_words(0)
+        for q in range(QUADRANTS):
             load_w4_scales(q)
-        load_w4()
-        load_tab(1)
-        load_u(1, 0, 256)
-        load_u(0, 256, 512)
-        load_u(1, 256, 384)
-        load_u(1, 384, 512)
-        gather_scales()
-        for i in range(6):
-            gather_x(i, 0, S)
-        quant_x("S", 0, 0, S)
-        gather_x(6, 0, S)
-        gather_x(7, 0, 256)
-        gather_x(7, 256, S)
-        quant_u("S", 0, 0, 256)
-        gather_tab(0)
-        quant_x("S", 1, 0, 256)
-        quant_x("S", 1, 256, S)
-        gather_tab(1)
-        quant_u("S", 1, 0, 256)
-        quant_u("S", 0, 256, 512)
-        quant_u("V", 1, 256, 384)
-        quant_u("V", 1, 384, 512)
-        for c in range(4):
-            mm("x", 0, c)
-        for c in range(2):
-            mm("u", 0, c)
-        for c in range(4):
-            mm("x", 1, c)
-        for c in range(2):
-            mm("u", 1, c)
-        y_first = sb("y_first", [P, 2 * S], F32, "u_raw0_256")
-        finish(0, y_first[:, 0:S])
-        finish(1, y_first[:, S : 2 * S])
-        mm("u", 1, 2)
-        mm("u", 0, 2)
-        mm("u", 0, 3)
-        mm("u", 1, 3)
-        y_last = sb("y_last", [P, 2 * S], F32)
+        nc.sync.dma_start(out=w4_sb[:].bitcast(I32), in_=w4_words.rearrange("a p x -> p a x").bitcast(I32))
+        load_tab_words(1)
+        load_u(1, 0, M_HALF)
+        load_u(0, M_HALF, M)
+        load_u(1, M_HALF, M_HALF + P)
+        load_u(1, M_HALF + P, M)
+
+        nc.vector.tensor_copy(v_scales[:], tab_scales[:].indirect(offs_sb[:]))
+        for i in range(PACK + 2):
+            gather_plane(i, 0, S)
+        quantise_xg(0, 0, S)
+        for i in range(PACK + 2, last_plane):
+            gather_plane(i, 0, S)
+        gather_plane(last_plane, 0, S_HALF)
+        gather_plane(last_plane, S_HALF, S)
+        quantise_u(nc.scalar.copy, 0, 0, M_HALF)
+        gather_tab_words(0)
+        quantise_xg(1, 0, S_HALF)
+        quantise_xg(1, S_HALF, S)
+        gather_tab_words(1)
+        quantise_u(nc.scalar.copy, 1, 0, M_HALF)
+        quantise_u(nc.scalar.copy, 0, M_HALF, M)
+        quantise_u(nc.vector.tensor_copy, 1, M_HALF, M_HALF + P)
+        quantise_u(nc.vector.tensor_copy, 1, M_HALF + P, M)
+
+        first_tiles = range(M_HALF // P)
+        for c in range(N_TILES):
+            multiply_heads(0, c)
+        for c in first_tiles:
+            multiply_table(0, c, False)
+        for c in range(N_TILES):
+            multiply_heads(1, c)
+        for c in first_tiles:
+            multiply_table(1, c, True)
+        y_first = sbuf("y_first", [P, 2 * S], F32, "u_raw0_%d" % M_HALF)
+        for c in first_tiles:
+            finish(c, y_first[:, S * c : S * (c + 1)])
+        multiply_table(1, 2, False)
+        multiply_table(0, 2, True)
+        multiply_table(0, 3, False)
+        multiply_table(1, 3, True)
+        y_last = sbuf("y_last", [P, 2 * S], F32)
         finish(2, y_last[:, 0:S])
         finish(3, y_last[:, S : 2 * S])

from contextlib import ExitStack

import concourse.mybir as mybir
from concourse.masks import make_identity

K, L, M, T, S = 1024, 1024, 512, 1024, 512
FLOPS = 2 * (K + L) * M * S

F32 = mybir.dt.float32
BF16 = mybir.dt.bfloat16
I32 = mybir.dt.int32
U32 = mybir.dt.uint32
U16 = mybir.dt.uint16
U8 = mybir.dt.uint8
FP8X4 = mybir.dt.float8_e4m3fn_x4
FP4X4 = mybir.dt.float4_e2m1fn_x4
GELU = mybir.ActivationFunctionType.Gelu_apprx_tanh
MULT = mybir.AluOpType.mult

P = 128
PACK = 4
K_PASS = P * PACK
PASSES = K // K_PASS
PLANES = PASSES * PACK
N_TILES = M // P
QUADRANTS = 4
QUADRANT = P // QUADRANTS
SCALE_ROWS = 4
PER_COLUMN = 16
LINE = 4
M_HALF = M // 2
S_HALF = S // 2


def tile_list_htab_gelu_kernel(tc, xT, w4_words, w4_scales, tab, u, wgt, b, offs, offs2, out):
    nc = tc.nc
    with ExitStack() as ctx:
        keep = ctx.enter_context(tc.tile_pool(name="keep", bufs=1))
        psum = ctx.enter_context(tc.psum_pool(name="psum", bufs=1))

        def sbuf(name, shape, dtype, tag=None):
            return keep.tile(shape, dtype, name=name, tag=tag or name, align_bytes=64)

        offs_sb = sbuf("offs_sb", [P, S // PER_COLUMN], U16)
        offs2_sb = sbuf("offs2_sb", [P, S // PER_COLUMN], U16)
        tab_words = [sbuf("tab_words%d" % a, [P, T], I32) for a in range(PASSES)]
        tab_scales = sbuf("tab_scales", [P, T], U8)
        w4_sb = sbuf("w4_sb", [P, PASSES, 2 * M], U8)
        w4_sc = sbuf("w4_sc", [P, PASSES, M], U8)
        wgt_sb = sbuf("wgt_sb", [P, S], F32)
        x_planes = [sbuf("x_plane%d" % i, [P, T], F32) for i in range(PLANES)]
        b_rows = sbuf("b_rows", [P, P], F32)
        ident = sbuf("ident", [P, P], F32)
        b_cols = sbuf("b_cols", [P, N_TILES], F32)
        warm = sbuf("warm", [P, 1], F32)
        picked = [sbuf("picked%d" % a, [P, PACK, S], F32) for a in range(PASSES)]
        xg_codes = [sbuf("xg_codes%d" % a, [P, S], U32) for a in range(PASSES)]
        v_codes = [sbuf("v_codes%d" % a, [P, S], U32) for a in range(PASSES)]
        v_scales = sbuf("v_scales", [P, S], U8)
        xg_scales = [sbuf("xg_scales%d" % a, [P, S], U8) for a in range(PASSES)]
        acc = [psum.tile([P, S], F32, name="acc%d" % c) for c in range(N_TILES)]
        b_ps = psum.tile([P, P], F32, name="b_ps")
        u_raw = {}
        u_codes = {}
        u_scales = {}

        def load_tab_scales(q):
            rows = tab[:, K_PASS * T :].rearrange("a (r t) -> a r t", t=T).bitcast(I32)
            first = QUADRANT * q + SCALE_ROWS
            nc.sync.dma_start(
                out=tab_scales[:].bitcast(I32)[first : first + PASSES * SCALE_ROWS, :],
                in_=rows[:, SCALE_ROWS * q : SCALE_ROWS * (q + 1), :],
            )

        def load_w4_scales(q):
            nc.sync.dma_start(
                out=w4_sc[:].bitcast(I32)[QUADRANT * q : QUADRANT * q + SCALE_ROWS, :, :],
                in_=w4_scales[:, SCALE_ROWS * q : SCALE_ROWS * (q + 1), :].rearrange("a r n -> r a n").bitcast(I32),
            )

        def load_tab_words(a):
            nc.sync.dma_start(out=tab_words[a][:], in_=tab[a, 0 : K_PASS * T].rearrange("(p x) -> p x", p=P).bitcast(I32))

        def load_plane(i):
            a, t = divmod(i, PACK)
            rows = xT[K_PASS * a : K_PASS * (a + 1), :].rearrange("(p t) x -> p t x", t=PACK)
            nc.sync.dma_start(out=x_planes[i][:], in_=rows[:, t, :])

        def load_u(a, n0, n1):
            u_raw[a, n0] = sbuf("u_raw%d_%d" % (a, n0), [P, PACK, n1 - n0], F32)
            rows = u[K_PASS * a : K_PASS * (a + 1), n0:n1].rearrange("(p t) n -> p t n", t=PACK)
            nc.sync.dma_start(out=u_raw[a, n0][:], in_=rows)

        def interleave(copy, name, src, width):
            woven = sbuf(name, [P, width, PACK], BF16)
            copy(woven[:].rearrange("p (c i) t -> p c t i", i=LINE), src.rearrange("p t (c i) -> p c t i", i=LINE))
            return woven[:].rearrange("p w t -> p (w t)")

        def gather_plane(i, j0, j1):
            a, t = divmod(i, PACK)
            window = x_planes[i][:].indirect(offs2_sb[:, j0 // PER_COLUMN : j1 // PER_COLUMN])
            nc.vector.tensor_tensor(picked[a][:, t, j0:j1], window, wgt_sb[:, j0:j1], MULT)

        def quantise_xg(a, j0, j1):
            woven = interleave(nc.scalar.copy, "x_woven%d_%d" % (a, j0), picked[a][:, :, j0:j1], j1 - j0)
            nc.vector.quantize_mx(out=xg_codes[a][:, j0:j1].bitcast(FP8X4), scales=xg_scales[a][:, j0:j1], in_=woven)

        def quantise_u(copy, a, n0, n1):
            woven = interleave(copy, "u_woven%d_%d" % (a, n0), u_raw[a, n0][:], n1 - n0)
            codes = sbuf("u_codes%d_%d" % (a, n0), [P, n1 - n0], U32)
            scales = sbuf("u_scales%d_%d" % (a, n0), [P, n1 - n0], U8)
            nc.vector.quantize_mx(out=codes[:].bitcast(FP8X4), scales=scales[:], in_=woven)
            for n in range(n0, n1, P):
                u_codes[a, n // P] = codes[:, n - n0 : n - n0 + P]
                u_scales[a, n // P] = scales[:, n - n0 : n - n0 + P]

        def gather_tab_words(a):
            nc.vector.tensor_copy(v_codes[a][:], tab_words[a][:].bitcast(U32).indirect(offs_sb[:]))

        def multiply_heads(a, c):
            nc.tensor.matmul_mx(
                out=acc[c][:],
                lhsT=w4_sb[:, a, 2 * P * c : 2 * P * (c + 1)].bitcast(FP4X4),
                lhsT_scale=w4_sc[:, a, P * c : P * (c + 1)],
                rhs=xg_codes[a][:].bitcast(FP8X4),
                rhs_scale=xg_scales[a][:],
                start=(a == 0),
                stop=False,
            )

        def multiply_table(a, c, closes):
            nc.tensor.matmul_mx(
                out=acc[c][:],
                lhsT=u_codes[a, c].bitcast(FP8X4),
                lhsT_scale=u_scales[a, c],
                rhs=v_codes[a][:].bitcast(FP8X4),
                rhs_scale=v_scales[SCALE_ROWS * (a + 1) : P, :],
                start=False,
                stop=closes,
            )

        def finish(c, y):
            nc.scalar.activation(y, acc[c][:], GELU, bias=b_cols[:, c : c + 1])
            nc.sync.dma_start(out=out[P * c : P * (c + 1), :], in_=y)

        nc.gpsimd.memset(tab_scales[:].bitcast(I32), 0)
        nc.vector.memset(w4_sc[:].bitcast(I32), 0)
        nc.vector.memset(b_rows[:], 0.0)
        make_identity(nc, ident[:])

        nc.sync.dma_start(offs_sb[:], offs)
        nc.sync.dma_start(out=wgt_sb[:], in_=wgt)
        for q in range(QUADRANTS):
            load_tab_scales(q)
        nc.scalar.activation(warm[:], ident[:, 0:1], GELU)
        load_plane(0)
        nc.sync.dma_start(offs2_sb[:], offs2)
        load_plane(1)
        nc.sync.dma_start(out=b_rows[0:N_TILES, :], in_=b.rearrange("(c p) -> c p", p=P))
        nc.tensor.transpose(b_ps[:], b_rows[:], ident[:])
        nc.scalar.copy(b_cols[:], b_ps[:, 0:N_TILES])
        last_plane = PLANES - 1
        for i in range(2, last_plane):
            load_plane(i)
        load_u(0, 0, M_HALF)
        load_plane(last_plane)
        load_tab_words(0)
        for q in range(QUADRANTS):
            load_w4_scales(q)
        nc.sync.dma_start(out=w4_sb[:].bitcast(I32), in_=w4_words.rearrange("a p x -> p a x").bitcast(I32))
        load_tab_words(1)
        load_u(1, 0, M_HALF)
        load_u(0, M_HALF, M)
        load_u(1, M_HALF, M_HALF + P)
        load_u(1, M_HALF + P, M)

        nc.vector.tensor_copy(v_scales[:], tab_scales[:].indirect(offs_sb[:]))
        for i in range(PACK + 2):
            gather_plane(i, 0, S)
        quantise_xg(0, 0, S)
        for i in range(PACK + 2, last_plane):
            gather_plane(i, 0, S)
        gather_plane(last_plane, 0, S_HALF)
        gather_plane(last_plane, S_HALF, S)
        quantise_u(nc.scalar.copy, 0, 0, M_HALF)
        gather_tab_words(0)
        quantise_xg(1, 0, S_HALF)
        quantise_xg(1, S_HALF, S)
        gather_tab_words(1)
        quantise_u(nc.scalar.copy, 1, 0, M_HALF)
        quantise_u(nc.scalar.copy, 0, M_HALF, M)
        quantise_u(nc.vector.tensor_copy, 1, M_HALF, M_HALF + P)
        quantise_u(nc.vector.tensor_copy, 1, M_HALF + P, M)

        first_tiles = range(M_HALF // P)
        for c in range(N_TILES):
            multiply_heads(0, c)
        for c in first_tiles:
            multiply_table(0, c, False)
        for c in range(N_TILES):
            multiply_heads(1, c)
        for c in first_tiles:
            multiply_table(1, c, True)
        y_first = sbuf("y_first", [P, 2 * S], F32, "u_raw0_%d" % M_HALF)
        for c in first_tiles:
            finish(c, y_first[:, S * c : S * (c + 1)])
        multiply_table(1, 2, False)
        multiply_table(0, 2, True)
        multiply_table(0, 3, False)
        multiply_table(1, 3, True)
        y_last = sbuf("y_last", [P, 2 * S], F32)
        finish(2, y_last[:, 0:S])
        finish(3, y_last[:, S : 2 * S])
